import numpy as np
import ml_dtypes


def mxq(x, axis, fmt="e4m3"):
    dtype, down = {"e4m3": (ml_dtypes.float8_e4m3fn, 7), "e5m2": (ml_dtypes.float8_e5m2, 14)}[fmt]
    v = np.moveaxis(np.asarray(x, np.float32).astype(ml_dtypes.bfloat16).astype(np.float64), axis, -1)
    blocks = v.reshape(v.shape[:-1] + (-1, 32))
    amax = np.abs(blocks).max(-1, keepdims=True)
    byte = np.maximum(np.where(amax > 0, np.frexp(amax)[1] - 1 + 127, 0) - down, 1)
    scale = np.exp2(byte - 127.0)
    codes = (blocks / scale).astype(np.float32).astype(dtype).astype(np.float64)
    return np.moveaxis((codes * scale).reshape(v.shape), -1, axis)


WIDE = False


def mx_kscale(k):
    if not WIDE:
        return np.ones(k)
    levels = np.array([24, -24, 12, -12, 0])
    if k % 512:
        return np.exp2(np.random.permutation(np.resize(levels, k // 32))).repeat(32)
    a = np.empty((k // 512, 16))
    for p in range(k // 512):
        a[p, :8] = np.random.permutation(np.resize(levels, 8))
        for g in range(8):
            far = levels[np.abs(levels - a[p, g]) >= 10]
            a[p, g + 8] = far[np.random.randint(len(far))]
    return np.exp2(a.ravel()).repeat(32)


def f64(x):
    return np.asarray(x).astype(np.float64)


E2M1 = np.array([0.0, 0.5, 1.0, 1.5, 2.0, 3.0, 4.0, 6.0, -0.0, -0.5, -1.0, -1.5, -2.0, -3.0, -4.0, -6.0])


def pack_weight(w, fmt):
    k, n = w.shape
    w = f64(np.asarray(w, np.float32).astype(ml_dtypes.bfloat16)).reshape(k // 32, 32, n)
    amax = np.abs(w).max(1)
    if fmt == "e4m3":
        byte = np.frexp(amax)[1] - 1 + 127 - 7
    else:
        mant, ex = np.frexp(amax / 6.0)
        byte = np.where(mant > 0.5, ex, ex - 1) + 127
    byte = np.clip(np.where(amax > 0, byte, 1), 1, 254)
    scaled = (w * np.exp2(127.0 - byte)[:, None, :]).reshape(k, n).astype(np.float32)
    by_word = np.ascontiguousarray(scaled.reshape(k // 512, 128, 4, n).transpose(0, 1, 3, 2))
    if fmt == "e4m3":
        words = by_word.astype(ml_dtypes.float8_e4m3fn).view(np.uint8)
    else:
        c = by_word.astype(ml_dtypes.float4_e2m1fn).view(np.uint8) & 0xF
        words = (c[..., 0::2] | (c[..., 1::2] << 4)).reshape(k // 512, 128, 2 * n)
    return np.ascontiguousarray(words), np.ascontiguousarray(byte.astype(np.uint8).reshape(k // 512, 16, n))


def unpack_weight(words, scales, fmt):
    g, _, n = scales.shape
    words = np.ascontiguousarray(words).reshape(g, 128, n, -1)
    if fmt == "e4m3":
        vals = words.view(ml_dtypes.float8_e4m3fn).astype(np.float64)
    else:
        nib = np.empty((g, 128, n, 4), np.uint8)
        nib[..., 0::2] = words & 0xF
        nib[..., 1::2] = words >> 4
        vals = E2M1[nib]
    vals = vals * np.repeat(np.exp2(scales.astype(np.float64) - 127.0), 8, axis=1)[..., None]
    return vals.transpose(0, 1, 3, 2).reshape(g * 512, n)


K, R, N, T = 1024, 512, 1024, 1536


def setup_inputs():
    n = np.random.standard_normal
    s = mx_kscale(K)[:, None]
    u = mx_kscale(R)[:, None]
    p_wb = pack_weight(0.7 * n((K, N)) / np.sqrt(K) / s, "e2m1")
    return {
        "x": (n((K, T)) * s).astype(np.float32),
        "wb_words": p_wb[0],
        "wb_scales": p_wb[1],
        "dn": (n((K, R)) / np.sqrt(K) / s).astype(np.float32),
        "upw": (n((R, N)) / np.sqrt(R) / u).astype(np.float32),
        "sm": (np.random.uniform(0.5, 2.0, R) * u[:, 0]).astype(np.float32),
        "x0": (n((N, T))).astype(np.float32),
        "b": (0.3 * n(N)).astype(np.float32),
        "xr": (n((N, T))).astype(np.float32),
    }


def reference(x, wb_words, wb_scales, dn, upw, sm, x0, b, xr):
    x_ = mxq(f64(x), 0, "e4m3")
    wb_ = unpack_weight(wb_words, wb_scales, "e2m1")
    dn_ = mxq(f64(dn), 0, "e4m3")
    upw_ = mxq(f64(upw), 0, "e4m3")
    hs = dn_.T @ x_
    h = f64(sm)[:, None] * np.tanh(hs)
    h_ = mxq(h, 0, "e4m3")
    y = wb_.T @ x_ + upw_.T @ h_
    return f64(x0) * (y + f64(b)[:, None]) + f64(xr)

@@ -1,0 +1,253 @@
+from contextlib import ExitStack
+
+import concourse.mybir as mybir
+
+K, R, N, T = 1024, 512, 1024, 1536
+FLOPS = 2 * T * (K * R + K * N + R * N)
+
+F32 = mybir.dt.float32
+BF16 = mybir.dt.bfloat16
+I32 = mybir.dt.int32
+U32 = mybir.dt.uint32
+U8 = mybir.dt.uint8
+FP8X4 = mybir.dt.float8_e4m3fn_x4
+FP4X4 = mybir.dt.float4_e2m1fn_x4
+ADD = mybir.AluOpType.add
+MULT = mybir.AluOpType.mult
+TANH = mybir.ActivationFunctionType.Tanh
+
+P = 128
+PACK = 4
+K_PASS = P * PACK
+PASSES = K // K_PASS
+HALF = T // 2
+UNIT = 256
+UNITS_PER_HALF = HALF // UNIT
+BANK = 512
+N_TILES = N // P
+OWN_TILES = N_TILES - 2
+
+
+def tile_mix_cross_tanh_kernel(
+    tc, x, wb_words, wb_scales, dn, upw, sm, x0, b, xr, out
+):
+    nc = tc.nc
+
+    with ExitStack() as ctx:
+        keep = ctx.enter_context(tc.tile_pool(name="keep", bufs=1))
+        stage = ctx.enter_context(tc.tile_pool(name="stage", bufs=1))
+        psum = ctx.enter_context(tc.psum_pool(name="psum", bufs=1))
+        ctx.enter_context(tc.manual_schedule())
+
+        def codes_and_scales(name, width):
+            codes = keep.tile([P, width], U32, name=name + "_codes", align_bytes=64)
+            scales = keep.tile([P, width], U8, name=name + "_scales", align_bytes=64)
+            return codes, scales
+
+        x_mx = [codes_and_scales("x%d" % a, T) for a in range(PASSES)]
+        dn_mx = [codes_and_scales("dn%d" % a, R) for a in range(PASSES)]
+        up_mx = codes_and_scales("up", N)
+        h_mx = codes_and_scales("h", T)
+
+        wb_plane = keep.tile([P, PASSES, N], U8, align_bytes=64)
+        nc.vector.memset(wb_plane[:].rearrange("p a n -> p (a n)").bitcast(I32), 0)
+
+        dn_raw = []
+        for a in range(PASSES):
+            raw = keep.tile([P, PACK, R], F32, name="dn_raw%d" % a)
+            nc.sync.dma_start(
+                out=raw[:], in_=dn[a * K_PASS : (a + 1) * K_PASS, :].rearrange("(p i) r -> p i r", i=PACK)
+            )
+            dn_raw.append(raw)
+
+        sm_col = keep.tile([P, PACK], F32)
+        nc.scalar.dma_start(out=sm_col[:], in_=sm.rearrange("(p j) -> p j", j=PACK))
+        for q in range(4):
+            nc.scalar.dma_start(
+                out=wb_plane[32 * q : 32 * q + 4, :, :].bitcast(I32),
+                in_=wb_scales[:, 4 * q : 4 * q + 4, :].rearrange("a r n -> r a n").bitcast(I32),
+            )
+        b_col = keep.tile([P, N_TILES], F32)
+        with nc.allow_non_contiguous_dma(reason="one bias value for each partition and output tile"):
+            nc.scalar.dma_start(out=b_col[:], in_=b.rearrange("(c p) -> p c", p=P))
+
+        x_raw = {}
+        for half in range(2):
+            for a in range(PASSES):
+                raw = stage.tile([P, PACK, HALF], F32, name="x_raw", tag="big", bufs=4)
+                nc.sync.dma_start(
+                    out=raw[:],
+                    in_=x[a * K_PASS : (a + 1) * K_PASS, half * HALF : (half + 1) * HALF].rearrange(
+                        "(p i) t -> p i t", i=PACK
+                    ),
+                )
+                x_raw[half, a] = raw
+
+        up_raw = keep.tile([P, PACK, N], F32)
+        nc.sync.dma_start(out=up_raw[:], in_=upw.rearrange("(p i) n -> p i n", i=PACK))
+        wb_codes = keep.tile([P, PASSES, 2 * N], U8, align_bytes=64)
+        nc.sync.dma_start(out=wb_codes[:], in_=wb_words.rearrange("a p n -> p a n"))
+
+        x0_sb, xr_sb = [], []
+
+        def load_features(nt):
+            for source, tiles, name in ((x0, x0_sb, "x0_"), (xr, xr_sb, "xr_")):
+                if nt < OWN_TILES:
+                    rows = keep.tile([P, T], F32, name=name + str(nt))
+                else:
+                    rows = stage.tile([P, T], F32, name=name + str(nt), tag="big", bufs=4)
+                nc.sync.dma_start(out=rows[:], in_=source[nt * P : (nt + 1) * P, :])
+                tiles.append(rows)
+
+        for nt in range(OWN_TILES):
+            load_features(nt)
+
+        def quantize(mx, start, grouped, width):
+            codes, scales = mx
+            cols = slice(start, start + width)
+            nc.vector.quantize_mx(out=codes[:, cols].bitcast(FP8X4), scales=scales[:, cols], in_=grouped[:])
+
+        def interleave(raw, start, on_scalar):
+            grouped = stage.tile([P, UNIT * PACK], BF16, name="grouped", bufs=5, align_bytes=64)
+            dst = grouped[:].rearrange("p (c e i) -> p c i e", e=4, i=PACK)
+            src = raw[:, :, start : start + UNIT].rearrange("p i (c e) -> p c i e", e=4)
+            if on_scalar:
+                nc.scalar.copy(out=dst, in_=src)
+            else:
+                nc.vector.tensor_copy(out=dst, in_=src)
+            return grouped
+
+        def x_steps(half, a):
+            grouped = {}
+
+            def copy_step(u):
+                def run():
+                    grouped[u] = interleave(x_raw[half, a], u * UNIT, u == 1)
+
+                return run
+
+            def quantize_step(u):
+                return lambda: quantize(x_mx[a], half * HALF + u * UNIT, grouped[u], UNIT)
+
+            units = range(UNITS_PER_HALF)
+            return [copy_step(u) for u in units] + [quantize_step(u) for u in units]
+
+        tanh_sb = {}
+
+        def hidden(u):
+            th = stage.tile([P, UNIT * PACK], F32, name="th", bufs=UNITS_PER_HALF)
+            for blk in range(UNIT // P):
+                cols = slice(u * UNIT + blk * P, u * UNIT + (blk + 1) * P)
+                hs = psum.tile([P, PACK, P], F32, name="hs", bufs=2)
+                for j in range(PACK):
+                    for a in range(PASSES):
+                        nc.tensor.matmul_mx(
+                            out=hs[:, j, :],
+                            lhsT=dn_mx[a][0][:, j * P : (j + 1) * P].bitcast(FP8X4),
+                            lhsT_scale=dn_mx[a][1][:, j * P : (j + 1) * P],
+                            rhs=x_mx[a][0][:, cols].bitcast(FP8X4),
+                            rhs_scale=x_mx[a][1][:, cols],
+                            start=(a == 0),
+                            stop=(a == PASSES - 1),
+                        )
+                nc.scalar.activation(
+                    out=th[:, blk * BANK : (blk + 1) * BANK].rearrange("p (t j) -> p t j", j=PACK),
+                    in_=hs[:].rearrange("p j t -> p t j"),
+                    func=TANH,
+                )
+            tanh_sb[u] = th
+
+        def h_steps(half):
+            rounded = {}
+
+            def scale_step(u):
+                def run():
+                    h_bf = stage.tile([P, UNIT * PACK], BF16, name="h_bf", bufs=2, align_bytes=64)
+                    nc.vector.tensor_tensor(out=h_bf[:], in0=tanh_sb[u][:], in1=sm_wide[:], op=MULT)
+                    rounded[u] = h_bf
+
+                return run
+
+            def quantize_step(u):
+                return lambda: quantize(h_mx, u * UNIT, rounded[u], UNIT)
+
+            steps = []
+            for u in range(half * UNITS_PER_HALF, (half + 1) * UNITS_PER_HALF):
+                steps.extend([scale_step(u), quantize_step(u)])
+            return steps
+
+        def weave(first, second):
+            for i in range(max(len(first), len(second))):
+                if i < len(first):
+                    first[i]()
+                if i < len(second):
+                    second[i]()
+
+        sm_wide = keep.tile([P, UNIT * PACK], F32)
+        for a in range(PASSES):
+            dn_grouped = stage.tile([P, R * PACK], BF16, name="dn_grouped", bufs=2, align_bytes=64)
+            nc.vector.tensor_copy(
+                out=dn_grouped[:].rearrange("p (j m i) -> p m i j", j=PACK, i=PACK),
+                in_=dn_raw[a][:].rearrange("p i (m j) -> p m i j", j=PACK),
+            )
+            if a == 0:
+                nc.vector.tensor_copy(
+                    out=sm_wide[:].rearrange("p (t j) -> p t j", j=PACK),
+                    in_=sm_col[:].unsqueeze(1).to_broadcast([P, UNIT, PACK]),
+                )
+            quantize(dn_mx[a], 0, dn_grouped, R)
+
+        for a in range(PASSES):
+            weave(x_steps(0, a), [])
+        for u in range(UNITS_PER_HALF):
+            hidden(u)
+        weave(x_steps(1, 0), h_steps(0))
+        weave(x_steps(1, 1), [])
+        for nt in range(OWN_TILES, N_TILES):
+            load_features(nt)
+        for u in range(UNITS_PER_HALF, 2 * UNITS_PER_HALF):
+            hidden(u)
+        up_grouped = [interleave(up_raw, q * UNIT, q > 0) for q in range(N // UNIT)]
+        weave(h_steps(1), [lambda: quantize(up_mx, 0, up_grouped[0], UNIT)])
+
+        def finish(nt):
+            nc.vector.tensor_tensor(out=x0_sb[nt][:], in0=x0_sb[nt][:], in1=xr_sb[nt][:], op=ADD)
+            nc.sync.dma_start(out=out[nt * P : (nt + 1) * P, :], in_=x0_sb[nt][:])
+
+        for nt in range(N_TILES):
+            rows = slice(nt * P, (nt + 1) * P)
+            if nt + 1 < N // UNIT:
+                quantize(up_mx, (nt + 1) * UNIT, up_grouped[nt + 1], UNIT)
+            for c in range(T // BANK):
+                cols = slice(c * BANK, (c + 1) * BANK)
+                y = psum.tile([P, BANK], F32, name="y", bufs=6)
+                for a in range(PASSES):
+                    nc.tensor.matmul_mx(
+                        out=y[:],
+                        lhsT=wb_codes[:, a, 2 * nt * P : 2 * (nt + 1) * P].bitcast(FP4X4),
+                        lhsT_scale=wb_plane[:, a, rows],
+                        rhs=x_mx[a][0][:, cols].bitcast(FP8X4),
+                        rhs_scale=x_mx[a][1][:, cols],
+                        start=(a == 0),
+                        stop=False,
+                    )
+                nc.tensor.matmul_mx(
+                    out=y[:],
+                    lhsT=up_mx[0][:, rows].bitcast(FP8X4),
+                    lhsT_scale=up_mx[1][:, rows],
+                    rhs=h_mx[0][:, cols].bitcast(FP8X4),
+                    rhs_scale=h_mx[1][:, cols],
+                    start=False,
+                    stop=True,
+                )
+                nc.vector.scalar_tensor_tensor(
+                    out=x0_sb[nt][:, cols],
+                    in0=y[:],
+                    scalar=b_col[:, nt : nt + 1],
+                    in1=x0_sb[nt][:, cols],
+                    op0=ADD,
+                    op1=MULT,
+                )
+                if c == 0 and nt > 0:
+                    finish(nt - 1)
+        finish(N_TILES - 1)

@@ -20,12 +20,12 @@ P = 128
 PACK = 4
 K_PASS = P * PACK
 PASSES = K // K_PASS
-HALF = T // 2
 UNIT = 256
-UNITS_PER_HALF = HALF // UNIT
+UNITS = T // UNIT
 BANK = 512
 N_TILES = N // P
-OWN_TILES = N_TILES - 2
+LOAD_TILES = 2
+STORE_TILES = (4, 2, 1)
 
 
 def tile_mix_cross_tanh_kernel(
@@ -49,96 +49,82 @@ def tile_mix_cross_tanh_kernel(
         up_mx = codes_and_scales("up", N)
         h_mx = codes_and_scales("h", T)
 
-        wb_plane = keep.tile([P, PASSES, N], U8, align_bytes=64)
-        nc.vector.memset(wb_plane[:].rearrange("p a n -> p (a n)").bitcast(I32), 0)
+        wb_raw = keep.tile([P, PASSES, 2 * N], U8, name="wb_raw")
+        nc.sync.dma_start(out=wb_raw[:], in_=wb_words.rearrange("a p n -> p a n"))
 
-        dn_raw = []
-        for a in range(PASSES):
-            raw = keep.tile([P, PACK, R], F32, name="dn_raw%d" % a)
-            nc.sync.dma_start(
-                out=raw[:], in_=dn[a * K_PASS : (a + 1) * K_PASS, :].rearrange("(p i) r -> p i r", i=PACK)
-            )
-            dn_raw.append(raw)
+        def load_rows(source, a, raw):
+            rows = source[a * K_PASS : (a + 1) * K_PASS, :]
+            nc.sync.dma_start(out=raw[:], in_=rows.rearrange("(p k) c -> p k c", k=PACK))
+            return raw
 
-        sm_col = keep.tile([P, PACK], F32)
+        x_raw = [load_rows(x, 0, stage.tile([P, PACK, T], F32, name="x_first", tag="shared", bufs=1))]
+
+        plane_raw = keep.tile([P, PASSES, N], U8, name="plane_raw")
+        nc.vector.memset(plane_raw[:].rearrange("p a n -> p (a n)").bitcast(I32), 0)
+        sm_col = keep.tile([P, PACK], F32, name="sm_col")
         nc.scalar.dma_start(out=sm_col[:], in_=sm.rearrange("(p j) -> p j", j=PACK))
+        b_col = keep.tile([P, N_TILES], F32, name="b_col")
+        nc.scalar.dma_start(out=b_col[:], in_=b.rearrange("(p i) -> p i", i=N_TILES))
         for q in range(4):
             nc.scalar.dma_start(
-                out=wb_plane[32 * q : 32 * q + 4, :, :].bitcast(I32),
+                out=plane_raw[32 * q : 32 * q + 4, :, :].bitcast(I32),
                 in_=wb_scales[:, 4 * q : 4 * q + 4, :].rearrange("a r n -> r a n").bitcast(I32),
             )
-        b_col = keep.tile([P, N_TILES], F32)
-        with nc.allow_non_contiguous_dma(reason="one bias value for each partition and output tile"):
-            nc.scalar.dma_start(out=b_col[:], in_=b.rearrange("(c p) -> p c", p=P))
 
-        x_raw = {}
-        for half in range(2):
-            for a in range(PASSES):
-                raw = stage.tile([P, PACK, HALF], F32, name="x_raw", tag="big", bufs=4)
-                nc.sync.dma_start(
-                    out=raw[:],
-                    in_=x[a * K_PASS : (a + 1) * K_PASS, half * HALF : (half + 1) * HALF].rearrange(
-                        "(p i) t -> p i t", i=PACK
-                    ),
-                )
-                x_raw[half, a] = raw
+        x_raw.append(load_rows(x, 1, keep.tile([P, PACK, T], F32, name="x_second")))
+        dn_raw = [load_rows(dn, a, keep.tile([P, PACK, R], F32, name="dn_raw%d" % a)) for a in range(PASSES)]
+        up_raw = load_rows(upw, 0, keep.tile([P, PACK, N], F32, name="up_raw"))
 
-        up_raw = keep.tile([P, PACK, N], F32)
-        nc.sync.dma_start(out=up_raw[:], in_=upw.rearrange("(p i) n -> p i n", i=PACK))
-        wb_codes = keep.tile([P, PASSES, 2 * N], U8, align_bytes=64)
-        nc.sync.dma_start(out=wb_codes[:], in_=wb_words.rearrange("a p n -> p a n"))
+        x0_hbm = x0.rearrange("(p i) t -> p (i t)", i=N_TILES)
+        xr_hbm = xr.rearrange("(p i) t -> p (i t)", i=N_TILES)
+        out_hbm = out.rearrange("(p i) t -> p (i t)", i=N_TILES)
+        x0_sb = keep.tile([P, N_TILES * T], F32, name="x0_sb")
+        half = N_TILES // 2
+        xr_sb = [keep.tile([P, half * T], F32, name="xr_first")]
 
-        x0_sb, xr_sb = [], []
+        def load_features(first):
+            cols = slice(first * T, (first + LOAD_TILES) * T)
+            nc.sync.dma_start(out=x0_sb[:, cols], in_=x0_hbm[:, cols])
+            start = (first % half) * T
+            nc.sync.dma_start(out=xr_sb[first // half][:, start : start + LOAD_TILES * T], in_=xr_hbm[:, cols])
 
-        def load_features(nt):
-            for source, tiles, name in ((x0, x0_sb, "x0_"), (xr, xr_sb, "xr_")):
-                if nt < OWN_TILES:
-                    rows = keep.tile([P, T], F32, name=name + str(nt))
-                else:
-                    rows = stage.tile([P, T], F32, name=name + str(nt), tag="big", bufs=4)
-                nc.sync.dma_start(out=rows[:], in_=source[nt * P : (nt + 1) * P, :])
-                tiles.append(rows)
+        for first in range(0, half, LOAD_TILES):
+            load_features(first)
 
-        for nt in range(OWN_TILES):
-            load_features(nt)
-
-        def quantize(mx, start, grouped, width):
+        def quantize(mx, u, grouped):
             codes, scales = mx
-            cols = slice(start, start + width)
+            cols = slice(u * UNIT, (u + 1) * UNIT)
             nc.vector.quantize_mx(out=codes[:, cols].bitcast(FP8X4), scales=scales[:, cols], in_=grouped[:])
 
-        def interleave(raw, start, on_scalar):
-            grouped = stage.tile([P, UNIT * PACK], BF16, name="grouped", bufs=5, align_bytes=64)
-            dst = grouped[:].rearrange("p (c e i) -> p c i e", e=4, i=PACK)
-            src = raw[:, :, start : start + UNIT].rearrange("p i (c e) -> p c i e", e=4)
+        def round_copy(dst, src, on_scalar):
             if on_scalar:
                 nc.scalar.copy(out=dst, in_=src)
             else:
                 nc.vector.tensor_copy(out=dst, in_=src)
+
+        def interleave(raw, u, on_scalar):
+            grouped = stage.tile([P, UNIT * PACK], BF16, name="grouped", bufs=6, align_bytes=64)
+            round_copy(
+                grouped[:].rearrange("p (c e k) -> p c k e", e=4, k=PACK),
+                raw[:, :, u * UNIT : (u + 1) * UNIT].rearrange("p k (c e) -> p c k e", e=4),
+                on_scalar,
+            )
             return grouped
 
-        def x_steps(half, a):
-            grouped = {}
+        def interleave_dealt(raw, u, on_scalar):
+            grouped = stage.tile([P, UNIT * PACK], BF16, name="grouped", bufs=6, align_bytes=64)
+            round_copy(
+                grouped[:].rearrange("p (s m k) -> p m k s", m=P, k=PACK),
+                raw[:].rearrange("p k (m s) -> p m k s", m=P)[:, :, :, 2 * u : 2 * u + 2],
+                on_scalar,
+            )
+            return grouped
 
-            def copy_step(u):
-                def run():
-                    grouped[u] = interleave(x_raw[half, a], u * UNIT, u == 1)
-
-                return run
-
-            def quantize_step(u):
-                return lambda: quantize(x_mx[a], half * HALF + u * UNIT, grouped[u], UNIT)
-
-            units = range(UNITS_PER_HALF)
-            return [copy_step(u) for u in units] + [quantize_step(u) for u in units]
-
-        tanh_sb = {}
-
-        def hidden(u):
-            th = stage.tile([P, UNIT * PACK], F32, name="th", bufs=UNITS_PER_HALF)
+        def hidden_tanh(u):
+            th = stage.tile([P, UNIT * PACK], F32, name="th", bufs=3)
             for blk in range(UNIT // P):
                 cols = slice(u * UNIT + blk * P, u * UNIT + (blk + 1) * P)
-                hs = psum.tile([P, PACK, P], F32, name="hs", bufs=2)
+                hs = psum.tile([P, PACK, P], F32, name="hs", tag="bank", bufs=8)
                 for j in range(PACK):
                     for a in range(PASSES):
                         nc.tensor.matmul_mx(
@@ -155,77 +141,106 @@ def tile_mix_cross_tanh_kernel(
                     in_=hs[:].rearrange("p j t -> p t j"),
                     func=TANH,
                 )
-            tanh_sb[u] = th
+            return th
 
-        def h_steps(half):
-            rounded = {}
+        def h_scale(th):
+            h_bf = stage.tile([P, UNIT * PACK], BF16, name="h_bf", bufs=3, align_bytes=64)
+            nc.vector.tensor_tensor(out=h_bf[:], in0=th[:], in1=sm_wide[:], op=MULT)
+            return h_bf
 
-            def scale_step(u):
-                def run():
-                    h_bf = stage.tile([P, UNIT * PACK], BF16, name="h_bf", bufs=2, align_bytes=64)
-                    nc.vector.tensor_tensor(out=h_bf[:], in0=tanh_sb[u][:], in1=sm_wide[:], op=MULT)
-                    rounded[u] = h_bf
+        warm = keep.tile([P, PACK], F32, name="warm")
+        nc.scalar.activation(out=warm[:], in_=sm_col[:], func=TANH)
 
-                return run
+        wb_codes = keep.tile([P, PASSES, 2 * N], U8, name="wb_codes", align_bytes=64)
+        nc.vector.tensor_copy(
+            out=wb_codes[:].rearrange("p a (i m e) -> p a i m e", m=P, e=2),
+            in_=wb_raw[:].rearrange("p a (m i e) -> p a i m e", m=P, e=2),
+        )
+        wb_plane = keep.tile([P, PASSES, N], U8, name="wb_plane", align_bytes=64)
+        nc.vector.tensor_copy(
+            out=wb_plane[:].rearrange("p a (i m) -> p a i m", m=P),
+            in_=plane_raw[:].rearrange("p a (m i) -> p a i m", m=P),
+        )
+        sm_wide = keep.tile([P, UNIT * PACK], F32, name="sm_wide")
+        nc.vector.tensor_copy(
+            out=sm_wide[:].rearrange("p (t j) -> p t j", j=PACK),
+            in_=sm_col[:].unsqueeze(1).to_broadcast([P, UNIT, PACK]),
+        )
 
-            def quantize_step(u):
-                return lambda: quantize(h_mx, u * UNIT, rounded[u], UNIT)
+        def prepare_pairs(pairs):
+            waiting = None
+            for copy_unit, raw, mx, u in pairs:
+                on_vector = copy_unit(raw, u, False)
+                on_scalar = copy_unit(raw, u + 1, True)
+                if waiting:
+                    quantize(*waiting)
+                quantize(mx, u, on_vector)
+                waiting = (mx, u + 1, on_scalar)
+            return waiting
 
-            steps = []
-            for u in range(half * UNITS_PER_HALF, (half + 1) * UNITS_PER_HALF):
-                steps.extend([scale_step(u), quantize_step(u)])
-            return steps
+        quantize(*prepare_pairs([(interleave, x_raw[0], x_mx[0], u) for u in range(0, UNITS, 2)]))
+        last_dn = prepare_pairs(
+            [(interleave, x_raw[1], x_mx[1], u) for u in range(0, UNITS - 2, 2)]
+            + [(interleave_dealt, dn_raw[a], dn_mx[a], 0) for a in range(PASSES)]
+        )
+        quantize(*last_dn)
+        late = [(x_mx[1], u, interleave(x_raw[1], u, False)) for u in range(UNITS - 2, UNITS)]
+        for unit in late:
+            quantize(*unit)
 
-        def weave(first, second):
-            for i in range(max(len(first), len(second))):
-                if i < len(first):
-                    first[i]()
-                if i < len(second):
-                    second[i]()
+        xr_sb.append(stage.tile([P, half * T], F32, name="xr_second", tag="shared", bufs=1))
+        for first in range(half, N_TILES, LOAD_TILES):
+            load_features(first)
 
-        sm_wide = keep.tile([P, UNIT * PACK], F32)
-        for a in range(PASSES):
-            dn_grouped = stage.tile([P, R * PACK], BF16, name="dn_grouped", bufs=2, align_bytes=64)
-            nc.vector.tensor_copy(
-                out=dn_grouped[:].rearrange("p (j m i) -> p m i j", j=PACK, i=PACK),
-                in_=dn_raw[a][:].rearrange("p i (m j) -> p m i j", j=PACK),
+        up_grouped = {}
+        rounded = None
+        for u in range(UNITS):
+            th = hidden_tanh(u)
+            if u == 4:
+                up_grouped[0] = interleave_dealt(up_raw, 0, True)
+            if u == UNITS - 1:
+                quantize(up_mx, 0, up_grouped[0])
+            previous, rounded = rounded, h_scale(th)
+            if previous is not None:
+                quantize(h_mx, u - 1, previous)
+        for q in range(1, N // UNIT):
+            up_grouped[q] = interleave_dealt(up_raw, q, True)
+        quantize(h_mx, UNITS - 1, rounded)
+
+        store_from = {}
+        first = 0
+        for count in STORE_TILES:
+            store_from[first + count - 1] = first
+            first = first + count
+
+        def add_residual(i, start, stop):
+            cols = slice(i * T + start, i * T + stop)
+            offset = (i % half) * T
+            nc.vector.tensor_tensor(
+                out=x0_sb[:, cols], in0=x0_sb[:, cols], in1=xr_sb[i // half][:, offset + start : offset + stop], op=ADD
             )
-            if a == 0:
-                nc.vector.tensor_copy(
-                    out=sm_wide[:].rearrange("p (t j) -> p t j", j=PACK),
-                    in_=sm_col[:].unsqueeze(1).to_broadcast([P, UNIT, PACK]),
-                )
-            quantize(dn_mx[a], 0, dn_grouped, R)
 
-        for a in range(PASSES):
-            weave(x_steps(0, a), [])
-        for u in range(UNITS_PER_HALF):
-            hidden(u)
-        weave(x_steps(1, 0), h_steps(0))
-        weave(x_steps(1, 1), [])
-        for nt in range(OWN_TILES, N_TILES):
-            load_features(nt)
-        for u in range(UNITS_PER_HALF, 2 * UNITS_PER_HALF):
-            hidden(u)
-        up_grouped = [interleave(up_raw, q * UNIT, q > 0) for q in range(N // UNIT)]
-        weave(h_steps(1), [lambda: quantize(up_mx, 0, up_grouped[0], UNIT)])
+        def store(start, stop):
+            nc.sync.dma_start(out=out_hbm[:, start:stop], in_=x0_sb[:, start:stop])
 
-        def finish(nt):
-            nc.vector.tensor_tensor(out=x0_sb[nt][:], in0=x0_sb[nt][:], in1=xr_sb[nt][:], op=ADD)
-            nc.sync.dma_start(out=out[nt * P : (nt + 1) * P, :], in_=x0_sb[nt][:])
+        def finish(i):
+            add_residual(i, 0, T)
+            if i in store_from:
+                store(store_from[i] * T, (i + 1) * T)
 
-        for nt in range(N_TILES):
-            rows = slice(nt * P, (nt + 1) * P)
-            if nt + 1 < N // UNIT:
-                quantize(up_mx, (nt + 1) * UNIT, up_grouped[nt + 1], UNIT)
+        for i in range(N_TILES):
+            channels = slice(i * P, (i + 1) * P)
+            q, odd = divmod(i + 1, 2)
+            if not odd and q < N // UNIT:
+                quantize(up_mx, q, up_grouped[q])
             for c in range(T // BANK):
                 cols = slice(c * BANK, (c + 1) * BANK)
-                y = psum.tile([P, BANK], F32, name="y", bufs=6)
+                y = psum.tile([P, BANK], F32, name="y", tag="bank", bufs=8)
                 for a in range(PASSES):
                     nc.tensor.matmul_mx(
                         out=y[:],
-                        lhsT=wb_codes[:, a, 2 * nt * P : 2 * (nt + 1) * P].bitcast(FP4X4),
-                        lhsT_scale=wb_plane[:, a, rows],
+                        lhsT=wb_codes[:, a, 2 * i * P : 2 * (i + 1) * P].bitcast(FP4X4),
+                        lhsT_scale=wb_plane[:, a, channels],
                         rhs=x_mx[a][0][:, cols].bitcast(FP8X4),
                         rhs_scale=x_mx[a][1][:, cols],
                         start=(a == 0),
@@ -233,21 +248,20 @@ def tile_mix_cross_tanh_kernel(
                     )
                 nc.tensor.matmul_mx(
                     out=y[:],
-                    lhsT=up_mx[0][:, rows].bitcast(FP8X4),
-                    lhsT_scale=up_mx[1][:, rows],
+                    lhsT=up_mx[0][:, channels].bitcast(FP8X4),
+                    lhsT_scale=up_mx[1][:, channels],
                     rhs=h_mx[0][:, cols].bitcast(FP8X4),
                     rhs_scale=h_mx[1][:, cols],
                     start=False,
                     stop=True,
                 )
+                features = x0_sb[:, i * T + c * BANK : i * T + (c + 1) * BANK]
                 nc.vector.scalar_tensor_tensor(
-                    out=x0_sb[nt][:, cols],
-                    in0=y[:],
-                    scalar=b_col[:, nt : nt + 1],
-                    in1=x0_sb[nt][:, cols],
-                    op0=ADD,
-                    op1=MULT,
+                    out=features, in0=y[:], scalar=b_col[:, i : i + 1], in1=features, op0=ADD, op1=MULT
                 )
-                if c == 0 and nt > 0:
-                    finish(nt - 1)
-        finish(N_TILES - 1)
+                if c == 0 and i > 0:
+                    finish(i - 1)
+        last = N_TILES - 1
+        for start, stop in ((0, 2 * BANK), (2 * BANK, T)):
+            add_residual(last, start, stop)
+            store(last * T + start, last * T + stop)

@@ -14,17 +14,24 @@ FP8X4 = mybir.dt.float8_e4m3fn_x4
 FP4X4 = mybir.dt.float4_e2m1fn_x4
 ADD = mybir.AluOpType.add
 MULT = mybir.AluOpType.mult
+COPY = mybir.ActivationFunctionType.Copy
 TANH = mybir.ActivationFunctionType.Tanh
 
 P = 128
 PACK = 4
 K_PASS = P * PACK
 PASSES = K // K_PASS
+QUADRANTS = 4
+FP4_BYTES = 2
+LINE = 4
 UNIT = 256
-UNITS = T // UNIT
+X_UNITS = T // UNIT
+UP_UNITS = N // UNIT
 BANK = 512
+PSUM_BANKS = 8
 N_TILES = N // P
-LOAD_TILES = 2
+HALF_TILES = N_TILES // 2
+XR_TILES = 2
 STORE_TILES = (4, 2, 1)
 
 
@@ -39,92 +46,97 @@ def tile_mix_cross_tanh_kernel(
         psum = ctx.enter_context(tc.psum_pool(name="psum", bufs=1))
         ctx.enter_context(tc.manual_schedule())
 
-        def codes_and_scales(name, width):
+        def mx_operand(name, width):
             codes = keep.tile([P, width], U32, name=name + "_codes", align_bytes=64)
             scales = keep.tile([P, width], U8, name=name + "_scales", align_bytes=64)
             return codes, scales
 
-        x_mx = [codes_and_scales("x%d" % a, T) for a in range(PASSES)]
-        dn_mx = [codes_and_scales("dn%d" % a, R) for a in range(PASSES)]
-        up_mx = codes_and_scales("up", N)
-        h_mx = codes_and_scales("h", T)
+        x_mx = [mx_operand("x%d" % a, T) for a in range(PASSES)]
+        dn_mx = [mx_operand("dn%d" % a, R) for a in range(PASSES)]
+        up_mx = mx_operand("up", N)
+        h_mx = mx_operand("h", T)
 
-        wb_raw = keep.tile([P, PASSES, 2 * N], U8, name="wb_raw")
-        nc.sync.dma_start(out=wb_raw[:], in_=wb_words.rearrange("a p n -> p a n"))
+        wb_words_raw = keep.tile([P, PASSES, FP4_BYTES * N], U8, name="wb_words_raw")
+        nc.sync.dma_start(out=wb_words_raw[:], in_=wb_words.rearrange("a p n -> p a n"))
 
-        def load_rows(source, a, raw):
+        def load_pass(source, a, raw):
             rows = source[a * K_PASS : (a + 1) * K_PASS, :]
             nc.sync.dma_start(out=raw[:], in_=rows.rearrange("(p k) c -> p k c", k=PACK))
             return raw
 
-        x_raw = [load_rows(x, 0, stage.tile([P, PACK, T], F32, name="x_first", tag="shared", bufs=1))]
+        x_raw = [load_pass(x, 0, stage.tile([P, PACK, T], F32, name="x_raw0", tag="x_then_xr"))]
 
-        plane_raw = keep.tile([P, PASSES, N], U8, name="plane_raw")
-        nc.vector.memset(plane_raw[:].rearrange("p a n -> p (a n)").bitcast(I32), 0)
+        wb_scales_raw = keep.tile([P, PASSES, N], U8, name="wb_scales_raw")
+        nc.gpsimd.memset(wb_scales_raw[:].rearrange("p a n -> p (a n)").bitcast(I32), 0)
         sm_col = keep.tile([P, PACK], F32, name="sm_col")
         nc.scalar.dma_start(out=sm_col[:], in_=sm.rearrange("(p j) -> p j", j=PACK))
         b_col = keep.tile([P, N_TILES], F32, name="b_col")
         nc.scalar.dma_start(out=b_col[:], in_=b.rearrange("(p i) -> p i", i=N_TILES))
-        for q in range(4):
-            nc.scalar.dma_start(
-                out=plane_raw[32 * q : 32 * q + 4, :, :].bitcast(I32),
+        for q in range(QUADRANTS):
+            nc.gpsimd.dma_start(
+                out=wb_scales_raw[32 * q : 32 * q + 4, :, :].bitcast(I32),
                 in_=wb_scales[:, 4 * q : 4 * q + 4, :].rearrange("a r n -> r a n").bitcast(I32),
             )
 
-        x_raw.append(load_rows(x, 1, keep.tile([P, PACK, T], F32, name="x_second")))
-        dn_raw = [load_rows(dn, a, keep.tile([P, PACK, R], F32, name="dn_raw%d" % a)) for a in range(PASSES)]
-        up_raw = load_rows(upw, 0, keep.tile([P, PACK, N], F32, name="up_raw"))
+        x_raw.append(load_pass(x, 1, keep.tile([P, PACK, T], F32, name="x_raw1")))
+        dn_raw = [load_pass(dn, a, keep.tile([P, PACK, R], F32, name="dn_raw%d" % a)) for a in range(PASSES)]
+        up_raw = load_pass(upw, 0, keep.tile([P, PACK, N], F32, name="up_raw"))
 
         x0_hbm = x0.rearrange("(p i) t -> p (i t)", i=N_TILES)
         xr_hbm = xr.rearrange("(p i) t -> p (i t)", i=N_TILES)
         out_hbm = out.rearrange("(p i) t -> p (i t)", i=N_TILES)
         x0_sb = keep.tile([P, N_TILES * T], F32, name="x0_sb")
-        half = N_TILES // 2
-        xr_sb = [keep.tile([P, half * T], F32, name="xr_first")]
+        xr_halves = []
 
-        def load_features(first):
-            cols = slice(first * T, (first + LOAD_TILES) * T)
+        def load_features(xr_half):
+            base = len(xr_halves) * HALF_TILES * T
+            cols = slice(base, base + HALF_TILES * T)
             nc.sync.dma_start(out=x0_sb[:, cols], in_=x0_hbm[:, cols])
-            start = (first % half) * T
-            nc.sync.dma_start(out=xr_sb[first // half][:, start : start + LOAD_TILES * T], in_=xr_hbm[:, cols])
+            for start in range(0, HALF_TILES * T, XR_TILES * T):
+                stop = start + XR_TILES * T
+                nc.sync.dma_start(out=xr_half[:, start:stop], in_=xr_hbm[:, base + start : base + stop])
+            xr_halves.append(xr_half)
 
-        for first in range(0, half, LOAD_TILES):
-            load_features(first)
+        load_features(keep.tile([P, HALF_TILES * T], F32, name="xr_half0"))
+
+        def round_unit(pattern, source, on_scalar, **sizes):
+            grouped = stage.tile([P, UNIT * PACK], BF16, name="grouped", bufs=6, align_bytes=64)
+            target = grouped[:].rearrange(pattern, k=PACK, **sizes)
+            if on_scalar:
+                nc.scalar.copy(out=target, in_=source)
+            else:
+                nc.vector.tensor_copy(out=target, in_=source)
+            return grouped
+
+        def round_in_order(raw, u, on_scalar):
+            source = raw[:, :, u * UNIT : (u + 1) * UNIT].rearrange("p k (c e) -> p c k e", e=LINE)
+            return round_unit("p (c e k) -> p c k e", source, on_scalar, e=LINE)
+
+        def round_dealt(raw, u, on_scalar):
+            source = raw[:].rearrange("p k (m s) -> p m k s", m=P)[:, :, :, 2 * u : 2 * u + 2]
+            return round_unit("p (s m k) -> p m k s", source, on_scalar, m=P)
 
         def quantize(mx, u, grouped):
             codes, scales = mx
             cols = slice(u * UNIT, (u + 1) * UNIT)
             nc.vector.quantize_mx(out=codes[:, cols].bitcast(FP8X4), scales=scales[:, cols], in_=grouped[:])
 
-        def round_copy(dst, src, on_scalar):
-            if on_scalar:
-                nc.scalar.copy(out=dst, in_=src)
-            else:
-                nc.vector.tensor_copy(out=dst, in_=src)
-
-        def interleave(raw, u, on_scalar):
-            grouped = stage.tile([P, UNIT * PACK], BF16, name="grouped", bufs=6, align_bytes=64)
-            round_copy(
-                grouped[:].rearrange("p (c e k) -> p c k e", e=4, k=PACK),
-                raw[:, :, u * UNIT : (u + 1) * UNIT].rearrange("p k (c e) -> p c k e", e=4),
-                on_scalar,
-            )
-            return grouped
-
-        def interleave_dealt(raw, u, on_scalar):
-            grouped = stage.tile([P, UNIT * PACK], BF16, name="grouped", bufs=6, align_bytes=64)
-            round_copy(
-                grouped[:].rearrange("p (s m k) -> p m k s", m=P, k=PACK),
-                raw[:].rearrange("p k (m s) -> p m k s", m=P)[:, :, :, 2 * u : 2 * u + 2],
-                on_scalar,
-            )
-            return grouped
+        def prepare_pairs(pairs):
+            waiting = None
+            for round_step, raw, mx, u in pairs:
+                by_vector = round_step(raw, u, False)
+                by_scalar = round_step(raw, u + 1, True)
+                if waiting:
+                    quantize(*waiting)
+                quantize(mx, u, by_vector)
+                waiting = (mx, u + 1, by_scalar)
+            quantize(*waiting)
 
         def hidden_tanh(u):
             th = stage.tile([P, UNIT * PACK], F32, name="th", bufs=3)
-            for blk in range(UNIT // P):
-                cols = slice(u * UNIT + blk * P, u * UNIT + (blk + 1) * P)
-                hs = psum.tile([P, PACK, P], F32, name="hs", tag="bank", bufs=8)
+            for block in range(UNIT // P):
+                cols = slice(u * UNIT + block * P, u * UNIT + (block + 1) * P)
+                hs = psum.tile([P, PACK, P], F32, name="hs", tag="bank", bufs=PSUM_BANKS)
                 for j in range(PACK):
                     for a in range(PASSES):
                         nc.tensor.matmul_mx(
@@ -137,109 +149,85 @@ def tile_mix_cross_tanh_kernel(
                             stop=(a == PASSES - 1),
                         )
                 nc.scalar.activation(
-                    out=th[:, blk * BANK : (blk + 1) * BANK].rearrange("p (t j) -> p t j", j=PACK),
+                    out=th[:, block * BANK : (block + 1) * BANK].rearrange("p (t j) -> p t j", j=PACK),
                     in_=hs[:].rearrange("p j t -> p t j"),
                     func=TANH,
                 )
             return th
 
-        def h_scale(th):
-            h_bf = stage.tile([P, UNIT * PACK], BF16, name="h_bf", bufs=3, align_bytes=64)
-            nc.vector.tensor_tensor(out=h_bf[:], in0=th[:], in1=sm_wide[:], op=MULT)
-            return h_bf
-
-        warm = keep.tile([P, PACK], F32, name="warm")
-        nc.scalar.activation(out=warm[:], in_=sm_col[:], func=TANH)
-
-        wb_codes = keep.tile([P, PASSES, 2 * N], U8, name="wb_codes", align_bytes=64)
-        nc.vector.tensor_copy(
-            out=wb_codes[:].rearrange("p a (i m e) -> p a i m e", m=P, e=2),
-            in_=wb_raw[:].rearrange("p a (m i e) -> p a i m e", m=P, e=2),
+        sm_wide = keep.tile([P, P * PACK], F32, name="sm_wide")
+        nc.scalar.activation(
+            out=sm_wide[:].rearrange("p (t j) -> p t j", j=PACK),
+            in_=sm_col[:].unsqueeze(1).to_broadcast([P, P, PACK]),
+            func=COPY,
         )
+
+        wb_codes = keep.tile([P, PASSES, FP4_BYTES * N], U8, name="wb_codes", align_bytes=64)
+        nc.vector.tensor_copy(
+            out=wb_codes[:].rearrange("p a (i m e) -> p a i m e", m=P, e=FP4_BYTES),
+            in_=wb_words_raw[:].rearrange("p a (m i e) -> p a i m e", m=P, e=FP4_BYTES),
+        )
+
+        prepare_pairs([(round_in_order, x_raw[0], x_mx[0], u) for u in range(0, X_UNITS, 2)])
+
         wb_plane = keep.tile([P, PASSES, N], U8, name="wb_plane", align_bytes=64)
         nc.vector.tensor_copy(
             out=wb_plane[:].rearrange("p a (i m) -> p a i m", m=P),
-            in_=plane_raw[:].rearrange("p a (m i) -> p a i m", m=P),
-        )
-        sm_wide = keep.tile([P, UNIT * PACK], F32, name="sm_wide")
-        nc.vector.tensor_copy(
-            out=sm_wide[:].rearrange("p (t j) -> p t j", j=PACK),
-            in_=sm_col[:].unsqueeze(1).to_broadcast([P, UNIT, PACK]),
+            in_=wb_scales_raw[:].rearrange("p a (m i) -> p a i m", m=P),
         )
 
-        def prepare_pairs(pairs):
-            waiting = None
-            for copy_unit, raw, mx, u in pairs:
-                on_vector = copy_unit(raw, u, False)
-                on_scalar = copy_unit(raw, u + 1, True)
-                if waiting:
-                    quantize(*waiting)
-                quantize(mx, u, on_vector)
-                waiting = (mx, u + 1, on_scalar)
-            return waiting
-
-        quantize(*prepare_pairs([(interleave, x_raw[0], x_mx[0], u) for u in range(0, UNITS, 2)]))
-        last_dn = prepare_pairs(
-            [(interleave, x_raw[1], x_mx[1], u) for u in range(0, UNITS - 2, 2)]
-            + [(interleave_dealt, dn_raw[a], dn_mx[a], 0) for a in range(PASSES)]
+        prepare_pairs(
+            [(round_in_order, x_raw[1], x_mx[1], u) for u in range(0, X_UNITS - 2, 2)]
+            + [(round_dealt, dn_raw[a], dn_mx[a], 0) for a in range(PASSES)]
         )
-        quantize(*last_dn)
-        late = [(x_mx[1], u, interleave(x_raw[1], u, False)) for u in range(UNITS - 2, UNITS)]
-        for unit in late:
-            quantize(*unit)
+        last_pair = [(u, round_in_order(x_raw[1], u, False)) for u in (X_UNITS - 2, X_UNITS - 1)]
+        for u, grouped in last_pair:
+            quantize(x_mx[1], u, grouped)
 
-        xr_sb.append(stage.tile([P, half * T], F32, name="xr_second", tag="shared", bufs=1))
-        for first in range(half, N_TILES, LOAD_TILES):
-            load_features(first)
+        load_features(stage.tile([P, HALF_TILES * T], F32, name="xr_half1", tag="x_then_xr"))
 
-        up_grouped = {}
-        rounded = None
-        for u in range(UNITS):
+        up_grouped = []
+        h_rounded = []
+        for u in range(X_UNITS):
             th = hidden_tanh(u)
-            if u == 4:
-                up_grouped[0] = interleave_dealt(up_raw, 0, True)
-            if u == UNITS - 1:
+            if u == X_UNITS - 2:
+                up_grouped.append(round_dealt(up_raw, 0, True))
+            if u == X_UNITS - 1:
                 quantize(up_mx, 0, up_grouped[0])
-            previous, rounded = rounded, h_scale(th)
-            if previous is not None:
-                quantize(h_mx, u - 1, previous)
-        for q in range(1, N // UNIT):
-            up_grouped[q] = interleave_dealt(up_raw, q, True)
-        quantize(h_mx, UNITS - 1, rounded)
-
-        store_from = {}
-        first = 0
-        for count in STORE_TILES:
-            store_from[first + count - 1] = first
-            first = first + count
+            h_bf = stage.tile([P, UNIT * PACK], BF16, name="h_bf", bufs=3, align_bytes=64)
+            for start in range(0, UNIT * PACK, BANK):
+                part = slice(start, start + BANK)
+                nc.vector.tensor_tensor(out=h_bf[:, part], in0=th[:, part], in1=sm_wide[:], op=MULT)
+            h_rounded.append(h_bf)
+            if u > 0:
+                quantize(h_mx, u - 1, h_rounded[u - 1])
+        for u in range(1, UP_UNITS):
+            up_grouped.append(round_dealt(up_raw, u, True))
+        quantize(h_mx, X_UNITS - 1, h_rounded[-1])
 
         def add_residual(i, start, stop):
             cols = slice(i * T + start, i * T + stop)
-            offset = (i % half) * T
-            nc.vector.tensor_tensor(
-                out=x0_sb[:, cols], in0=x0_sb[:, cols], in1=xr_sb[i // half][:, offset + start : offset + stop], op=ADD
-            )
+            half, place = divmod(i, HALF_TILES)
+            residual = xr_halves[half][:, place * T + start : place * T + stop]
+            nc.vector.tensor_tensor(out=x0_sb[:, cols], in0=x0_sb[:, cols], in1=residual, op=ADD)
 
         def store(start, stop):
             nc.sync.dma_start(out=out_hbm[:, start:stop], in_=x0_sb[:, start:stop])
 
-        def finish(i):
-            add_residual(i, 0, T)
-            if i in store_from:
-                store(store_from[i] * T, (i + 1) * T)
+        store_start = {sum(STORE_TILES[: s + 1]) - 1: sum(STORE_TILES[:s]) for s in range(len(STORE_TILES))}
 
         for i in range(N_TILES):
             channels = slice(i * P, (i + 1) * P)
-            q, odd = divmod(i + 1, 2)
-            if not odd and q < N // UNIT:
-                quantize(up_mx, q, up_grouped[q])
+            next_unit, odd = divmod(i + 1, 2)
+            if not odd and next_unit < UP_UNITS:
+                quantize(up_mx, next_unit, up_grouped[next_unit])
             for c in range(T // BANK):
                 cols = slice(c * BANK, (c + 1) * BANK)
-                y = psum.tile([P, BANK], F32, name="y", tag="bank", bufs=8)
+                y = psum.tile([P, BANK], F32, name="y", tag="bank", bufs=PSUM_BANKS)
                 for a in range(PASSES):
                     nc.tensor.matmul_mx(
                         out=y[:],
-                        lhsT=wb_codes[:, a, 2 * i * P : 2 * (i + 1) * P].bitcast(FP4X4),
+                        lhsT=wb_codes[:, a, FP4_BYTES * i * P : FP4_BYTES * (i + 1) * P].bitcast(FP4X4),
                         lhsT_scale=wb_plane[:, a, channels],
                         rhs=x_mx[a][0][:, cols].bitcast(FP8X4),
                         rhs_scale=x_mx[a][1][:, cols],
@@ -260,8 +248,11 @@ def tile_mix_cross_tanh_kernel(
                     out=features, in0=y[:], scalar=b_col[:, i : i + 1], in1=features, op0=ADD, op1=MULT
                 )
                 if c == 0 and i > 0:
-                    finish(i - 1)
+                    add_residual(i - 1, 0, T)
+                    if i - 1 in store_start:
+                        store(store_start[i - 1] * T, i * T)
+
         last = N_TILES - 1
-        for start, stop in ((0, 2 * BANK), (2 * BANK, T)):
+        for start, stop in ((0, T - BANK), (T - BANK, T)):
             add_residual(last, start, stop)
             store(last * T + start, last * T + stop)

@@ -33,6 +33,7 @@ N_TILES = N // P
 HALF_TILES = N_TILES // 2
 XR_TILES = 2
 STORE_TILES = (4, 2, 1)
+GPSIMD_COLS = 256
 
 
 def tile_mix_cross_tanh_kernel(
@@ -67,13 +68,13 @@ def tile_mix_cross_tanh_kernel(
         x_raw = [load_pass(x, 0, stage.tile([P, PACK, T], F32, name="x_raw0", tag="x_then_xr"))]
 
         wb_scales_raw = keep.tile([P, PASSES, N], U8, name="wb_scales_raw")
-        nc.gpsimd.memset(wb_scales_raw[:].rearrange("p a n -> p (a n)").bitcast(I32), 0)
+        nc.vector.memset(wb_scales_raw[:].rearrange("p a n -> p (a n)").bitcast(I32), 0)
         sm_col = keep.tile([P, PACK], F32, name="sm_col")
         nc.scalar.dma_start(out=sm_col[:], in_=sm.rearrange("(p j) -> p j", j=PACK))
         b_col = keep.tile([P, N_TILES], F32, name="b_col")
         nc.scalar.dma_start(out=b_col[:], in_=b.rearrange("(p i) -> p i", i=N_TILES))
         for q in range(QUADRANTS):
-            nc.gpsimd.dma_start(
+            nc.scalar.dma_start(
                 out=wb_scales_raw[32 * q : 32 * q + 4, :, :].bitcast(I32),
                 in_=wb_scales[:, 4 * q : 4 * q + 4, :].rearrange("a r n -> r a n").bitcast(I32),
             )
@@ -205,11 +206,11 @@ def tile_mix_cross_tanh_kernel(
             up_grouped.append(round_dealt(up_raw, u, True))
         quantize(h_mx, X_UNITS - 1, h_rounded[-1])
 
-        def add_residual(i, start, stop):
+        def add_residual(engine, i, start, stop):
             cols = slice(i * T + start, i * T + stop)
             half, place = divmod(i, HALF_TILES)
             residual = xr_halves[half][:, place * T + start : place * T + stop]
-            nc.vector.tensor_tensor(out=x0_sb[:, cols], in0=x0_sb[:, cols], in1=residual, op=ADD)
+            engine.tensor_tensor(out=x0_sb[:, cols], in0=x0_sb[:, cols], in1=residual, op=ADD)
 
         def store(start, stop):
             nc.sync.dma_start(out=out_hbm[:, start:stop], in_=x0_sb[:, start:stop])
@@ -247,12 +248,15 @@ def tile_mix_cross_tanh_kernel(
                 nc.vector.scalar_tensor_tensor(
                     out=features, in0=y[:], scalar=b_col[:, i : i + 1], in1=features, op0=ADD, op1=MULT
                 )
-                if c == 0 and i > 0:
-                    add_residual(i - 1, 0, T)
-                    if i - 1 in store_start:
-                        store(store_start[i - 1] * T, i * T)
+                if c == 0:
+                    add_residual(nc.gpsimd, i, 0, GPSIMD_COLS)
+            if i > 0:
+                add_residual(nc.vector, i - 1, GPSIMD_COLS, T)
+                if i - 1 in store_start:
+                    store(store_start[i - 1] * T, i * T)
 
         last = N_TILES - 1
-        for start, stop in ((0, T - BANK), (T - BANK, T)):
-            add_residual(last, start, stop)
-            store(last * T + start, last * T + stop)
+        add_residual(nc.vector, last, GPSIMD_COLS, T - BANK)
+        store(last * T, (last + 1) * T - BANK)
+        add_residual(nc.vector, last, T - BANK, T)
+        store((last + 1) * T - BANK, (last + 1) * T)

from contextlib import ExitStack

import concourse.mybir as mybir

K, R, N, T = 1024, 512, 1024, 1536
FLOPS = 2 * T * (K * R + K * N + R * N)

F32 = mybir.dt.float32
BF16 = mybir.dt.bfloat16
I32 = mybir.dt.int32
U32 = mybir.dt.uint32
U8 = mybir.dt.uint8
FP8X4 = mybir.dt.float8_e4m3fn_x4
FP4X4 = mybir.dt.float4_e2m1fn_x4
ADD = mybir.AluOpType.add
MULT = mybir.AluOpType.mult
COPY = mybir.ActivationFunctionType.Copy
TANH = mybir.ActivationFunctionType.Tanh

P = 128
PACK = 4
K_PASS = P * PACK
PASSES = K // K_PASS
QUADRANTS = 4
FP4_BYTES = 2
LINE = 4
UNIT = 256
X_UNITS = T // UNIT
UP_UNITS = N // UNIT
BANK = 512
PSUM_BANKS = 8
N_TILES = N // P
HALF_TILES = N_TILES // 2
XR_TILES = 2
STORE_TILES = (4, 2, 1)
GPSIMD_COLS = 256


def tile_mix_cross_tanh_kernel(
    tc, x, wb_words, wb_scales, dn, upw, sm, x0, b, xr, out
):
    nc = tc.nc

    with ExitStack() as ctx:
        keep = ctx.enter_context(tc.tile_pool(name="keep", bufs=1))
        stage = ctx.enter_context(tc.tile_pool(name="stage", bufs=1))
        psum = ctx.enter_context(tc.psum_pool(name="psum", bufs=1))
        ctx.enter_context(tc.manual_schedule())

        def mx_operand(name, width):
            codes = keep.tile([P, width], U32, name=name + "_codes", align_bytes=64)
            scales = keep.tile([P, width], U8, name=name + "_scales", align_bytes=64)
            return codes, scales

        x_mx = [mx_operand("x%d" % a, T) for a in range(PASSES)]
        dn_mx = [mx_operand("dn%d" % a, R) for a in range(PASSES)]
        up_mx = mx_operand("up", N)
        h_mx = mx_operand("h", T)

        wb_words_raw = keep.tile([P, PASSES, FP4_BYTES * N], U8, name="wb_words_raw")
        nc.sync.dma_start(out=wb_words_raw[:], in_=wb_words.rearrange("a p n -> p a n"))

        def load_pass(source, a, raw):
            rows = source[a * K_PASS : (a + 1) * K_PASS, :]
            nc.sync.dma_start(out=raw[:], in_=rows.rearrange("(p k) c -> p k c", k=PACK))
            return raw

        x_raw = [load_pass(x, 0, stage.tile([P, PACK, T], F32, name="x_raw0", tag="x_then_xr"))]

        wb_scales_raw = keep.tile([P, PASSES, N], U8, name="wb_scales_raw")
        nc.vector.memset(wb_scales_raw[:].rearrange("p a n -> p (a n)").bitcast(I32), 0)
        sm_col = keep.tile([P, PACK], F32, name="sm_col")
        nc.scalar.dma_start(out=sm_col[:], in_=sm.rearrange("(p j) -> p j", j=PACK))
        b_col = keep.tile([P, N_TILES], F32, name="b_col")
        nc.scalar.dma_start(out=b_col[:], in_=b.rearrange("(p i) -> p i", i=N_TILES))
        for q in range(QUADRANTS):
            nc.scalar.dma_start(
                out=wb_scales_raw[32 * q : 32 * q + 4, :, :].bitcast(I32),
                in_=wb_scales[:, 4 * q : 4 * q + 4, :].rearrange("a r n -> r a n").bitcast(I32),
            )

        x_raw.append(load_pass(x, 1, keep.tile([P, PACK, T], F32, name="x_raw1")))
        dn_raw = [load_pass(dn, a, keep.tile([P, PACK, R], F32, name="dn_raw%d" % a)) for a in range(PASSES)]
        up_raw = load_pass(upw, 0, keep.tile([P, PACK, N], F32, name="up_raw"))

        x0_hbm = x0.rearrange("(p i) t -> p (i t)", i=N_TILES)
        xr_hbm = xr.rearrange("(p i) t -> p (i t)", i=N_TILES)
        out_hbm = out.rearrange("(p i) t -> p (i t)", i=N_TILES)
        x0_sb = keep.tile([P, N_TILES * T], F32, name="x0_sb")
        xr_halves = []

        def load_features(xr_half):
            base = len(xr_halves) * HALF_TILES * T
            cols = slice(base, base + HALF_TILES * T)
            nc.sync.dma_start(out=x0_sb[:, cols], in_=x0_hbm[:, cols])
            for start in range(0, HALF_TILES * T, XR_TILES * T):
                stop = start + XR_TILES * T
                nc.sync.dma_start(out=xr_half[:, start:stop], in_=xr_hbm[:, base + start : base + stop])
            xr_halves.append(xr_half)

        load_features(keep.tile([P, HALF_TILES * T], F32, name="xr_half0"))

        def round_unit(pattern, source, on_scalar, **sizes):
            grouped = stage.tile([P, UNIT * PACK], BF16, name="grouped", bufs=6, align_bytes=64)
            target = grouped[:].rearrange(pattern, k=PACK, **sizes)
            if on_scalar:
                nc.scalar.copy(out=target, in_=source)
            else:
                nc.vector.tensor_copy(out=target, in_=source)
            return grouped

        def round_in_order(raw, u, on_scalar):
            source = raw[:, :, u * UNIT : (u + 1) * UNIT].rearrange("p k (c e) -> p c k e", e=LINE)
            return round_unit("p (c e k) -> p c k e", source, on_scalar, e=LINE)

        def round_dealt(raw, u, on_scalar):
            source = raw[:].rearrange("p k (m s) -> p m k s", m=P)[:, :, :, 2 * u : 2 * u + 2]
            return round_unit("p (s m k) -> p m k s", source, on_scalar, m=P)

        def quantize(mx, u, grouped):
            codes, scales = mx
            cols = slice(u * UNIT, (u + 1) * UNIT)
            nc.vector.quantize_mx(out=codes[:, cols].bitcast(FP8X4), scales=scales[:, cols], in_=grouped[:])

        def prepare_pairs(pairs):
            waiting = None
            for round_step, raw, mx, u in pairs:
                by_vector = round_step(raw, u, False)
                by_scalar = round_step(raw, u + 1, True)
                if waiting:
                    quantize(*waiting)
                quantize(mx, u, by_vector)
                waiting = (mx, u + 1, by_scalar)
            quantize(*waiting)

        def hidden_tanh(u):
            th = stage.tile([P, UNIT * PACK], F32, name="th", bufs=3)
            for block in range(UNIT // P):
                cols = slice(u * UNIT + block * P, u * UNIT + (block + 1) * P)
                hs = psum.tile([P, PACK, P], F32, name="hs", tag="bank", bufs=PSUM_BANKS)
                for j in range(PACK):
                    for a in range(PASSES):
                        nc.tensor.matmul_mx(
                            out=hs[:, j, :],
                            lhsT=dn_mx[a][0][:, j * P : (j + 1) * P].bitcast(FP8X4),
                            lhsT_scale=dn_mx[a][1][:, j * P : (j + 1) * P],
                            rhs=x_mx[a][0][:, cols].bitcast(FP8X4),
                            rhs_scale=x_mx[a][1][:, cols],
                            start=(a == 0),
                            stop=(a == PASSES - 1),
                        )
                nc.scalar.activation(
                    out=th[:, block * BANK : (block + 1) * BANK].rearrange("p (t j) -> p t j", j=PACK),
                    in_=hs[:].rearrange("p j t -> p t j"),
                    func=TANH,
                )
            return th

        sm_wide = keep.tile([P, P * PACK], F32, name="sm_wide")
        nc.scalar.activation(
            out=sm_wide[:].rearrange("p (t j) -> p t j", j=PACK),
            in_=sm_col[:].unsqueeze(1).to_broadcast([P, P, PACK]),
            func=COPY,
        )

        wb_codes = keep.tile([P, PASSES, FP4_BYTES * N], U8, name="wb_codes", align_bytes=64)
        nc.vector.tensor_copy(
            out=wb_codes[:].rearrange("p a (i m e) -> p a i m e", m=P, e=FP4_BYTES),
            in_=wb_words_raw[:].rearrange("p a (m i e) -> p a i m e", m=P, e=FP4_BYTES),
        )

        prepare_pairs([(round_in_order, x_raw[0], x_mx[0], u) for u in range(0, X_UNITS, 2)])

        wb_plane = keep.tile([P, PASSES, N], U8, name="wb_plane", align_bytes=64)
        nc.vector.tensor_copy(
            out=wb_plane[:].rearrange("p a (i m) -> p a i m", m=P),
            in_=wb_scales_raw[:].rearrange("p a (m i) -> p a i m", m=P),
        )

        prepare_pairs(
            [(round_in_order, x_raw[1], x_mx[1], u) for u in range(0, X_UNITS - 2, 2)]
            + [(round_dealt, dn_raw[a], dn_mx[a], 0) for a in range(PASSES)]
        )
        last_pair = [(u, round_in_order(x_raw[1], u, False)) for u in (X_UNITS - 2, X_UNITS - 1)]
        for u, grouped in last_pair:
            quantize(x_mx[1], u, grouped)

        load_features(stage.tile([P, HALF_TILES * T], F32, name="xr_half1", tag="x_then_xr"))

        up_grouped = []
        h_rounded = []
        for u in range(X_UNITS):
            th = hidden_tanh(u)
            if u == X_UNITS - 2:
                up_grouped.append(round_dealt(up_raw, 0, True))
            if u == X_UNITS - 1:
                quantize(up_mx, 0, up_grouped[0])
            h_bf = stage.tile([P, UNIT * PACK], BF16, name="h_bf", bufs=3, align_bytes=64)
            for start in range(0, UNIT * PACK, BANK):
                part = slice(start, start + BANK)
                nc.vector.tensor_tensor(out=h_bf[:, part], in0=th[:, part], in1=sm_wide[:], op=MULT)
            h_rounded.append(h_bf)
            if u > 0:
                quantize(h_mx, u - 1, h_rounded[u - 1])
        for u in range(1, UP_UNITS):
            up_grouped.append(round_dealt(up_raw, u, True))
        quantize(h_mx, X_UNITS - 1, h_rounded[-1])

        def add_residual(engine, i, start, stop):
            cols = slice(i * T + start, i * T + stop)
            half, place = divmod(i, HALF_TILES)
            residual = xr_halves[half][:, place * T + start : place * T + stop]
            engine.tensor_tensor(out=x0_sb[:, cols], in0=x0_sb[:, cols], in1=residual, op=ADD)

        def store(start, stop):
            nc.sync.dma_start(out=out_hbm[:, start:stop], in_=x0_sb[:, start:stop])

        store_start = {sum(STORE_TILES[: s + 1]) - 1: sum(STORE_TILES[:s]) for s in range(len(STORE_TILES))}

        for i in range(N_TILES):
            channels = slice(i * P, (i + 1) * P)
            next_unit, odd = divmod(i + 1, 2)
            if not odd and next_unit < UP_UNITS:
                quantize(up_mx, next_unit, up_grouped[next_unit])
            for c in range(T // BANK):
                cols = slice(c * BANK, (c + 1) * BANK)
                y = psum.tile([P, BANK], F32, name="y", tag="bank", bufs=PSUM_BANKS)
                for a in range(PASSES):
                    nc.tensor.matmul_mx(
                        out=y[:],
                        lhsT=wb_codes[:, a, FP4_BYTES * i * P : FP4_BYTES * (i + 1) * P].bitcast(FP4X4),
                        lhsT_scale=wb_plane[:, a, channels],
                        rhs=x_mx[a][0][:, cols].bitcast(FP8X4),
                        rhs_scale=x_mx[a][1][:, cols],
                        start=(a == 0),
                        stop=False,
                    )
                nc.tensor.matmul_mx(
                    out=y[:],
                    lhsT=up_mx[0][:, channels].bitcast(FP8X4),
                    lhsT_scale=up_mx[1][:, channels],
                    rhs=h_mx[0][:, cols].bitcast(FP8X4),
                    rhs_scale=h_mx[1][:, cols],
                    start=False,
                    stop=True,
                )
                features = x0_sb[:, i * T + c * BANK : i * T + (c + 1) * BANK]
                nc.vector.scalar_tensor_tensor(
                    out=features, in0=y[:], scalar=b_col[:, i : i + 1], in1=features, op0=ADD, op1=MULT
                )
                if c == 0:
                    add_residual(nc.gpsimd, i, 0, GPSIMD_COLS)
            if i > 0:
                add_residual(nc.vector, i - 1, GPSIMD_COLS, T)
                if i - 1 in store_start:
                    store(store_start[i - 1] * T, i * T)

        last = N_TILES - 1
        add_residual(nc.vector, last, GPSIMD_COLS, T - BANK)
        store(last * T, (last + 1) * T - BANK)
        add_residual(nc.vector, last, T - BANK, T)
        store((last + 1) * T - BANK, (last + 1) * T)
